import numpy as np
CORES = [0,1,8,9,16,17,24,25,32,33,40,41,48,49,56,57,64,65,72,73,80,81,88,89,96,97,104,105,112,113,120,121,128,129,136,137,144,145,152,153,160,161,168,169,176,177,184,185,192,193,200,201,208,209,216,217,224,225,232,233,240,241,248,249,256,257,264,265,272,273,280,281,288,289,296,297,304,305,312,313,320,321,328,329,336,337,344,345,352,353,360,361,368,369,376,377,384,385,392,393,400,401,408,409,416,417,424,425,432,433,440,441,448,449,456,457,464,465,472,473,480,481,488,489,496,497,504,505]
N = 128
ROUNDS = 8
PERM = [[i, (i + 64) % N] for i in range(N)]
def setup_inputs(rng):
    return {"x": rng.standard_normal((N, ROUNDS, 128, 64), dtype=np.float32)}
def reference(x):
    y = np.empty_like(x)
    for s, d in PERM:
        y[d] = x[s]
    return {"y": y}

@@ -1,0 +1,55 @@
+from concourse.bass import DstId, RemoteDMATransfer
+
+ROUNDS = 8
+PHASES = ROUNDS // 2
+
+SCRATCH = {
+    "own": ("dram", [2, 128, 64], "float32"),
+    "relay": ("dram", [2, 128, 64], "float32"),
+}
+SEMAPHORES = ["loaded", "stored", "sent", "passing", "landed"]
+
+LO, HI = 0x0F, 0xF0
+PER_CALL = 8
+
+
+def rank_program(g, core, T, topo):
+    if T.rank_of(core) is None:
+        return
+    h, place = topo.host(core), core % 128
+
+    def at(host):
+        return host * 128 + place
+
+    def transfer(dst_core, mask, sem, src, dst):
+        rid, pid = topo.addr(dst_core, core)
+        return RemoteDMATransfer(dst_ids=[DstId(rid=rid, pnc=pid)], dma_engine_mask=mask, remote_sem=sem,
+                                 src=src, dst=dst)
+
+    even_relay, odd_relay = (at(3), at(1)) if h % 2 == 0 else (at(0), at(2))
+    side = h // 2
+    client0, client1 = (at(1), at(3)) if h % 2 == 0 else (at(0), at(2))
+    parity = 0 if h in (0, 3) else 1
+
+    for p in range(PHASES):
+        if p:
+            g.wait_ge(T.sem.landed, PER_CALL * p)
+            g.dma_start(T.y[2 * p - 2:2 * p], T.own[:]).then_inc(T.sem.stored, 16)
+            g.wait_ge(T.sem.stored, 16 * p)
+        g.dma_start(T.own[:], T.x[2 * p:2 * p + 2]).then_inc(T.sem.loaded, 16)
+        g.wait_ge(T.sem.loaded, 16 * (p + 1))
+        slot = (side + p) % 2
+        g.remote_dma_fused([
+            transfer(even_relay, LO, T.sem.passing, T.own[0], T.relay[slot]),
+            transfer(odd_relay, HI, T.sem.passing, T.own[1], T.relay[slot]),
+        ], local_sem=T.sem.sent)
+        g.wait_ge(T.sem.passing, PER_CALL * (p + 1))
+        g.remote_dma_fused([
+            transfer(client1, LO, T.sem.landed, T.relay[p % 2], T.own[parity]),
+            transfer(client0, HI, T.sem.landed, T.relay[(p + 1) % 2], T.own[parity]),
+        ], local_sem=T.sem.sent)
+
+    g.wait_ge(T.sem.landed, PER_CALL * PHASES)
+    g.dma_start(T.y[ROUNDS - 2:ROUNDS], T.own[:]).then_inc(T.sem.stored, 16)
+    g.wait_ge(T.sem.stored, 16 * PHASES)
+    g.wait_ge(T.sem.sent, 2 * PER_CALL * PHASES)

@@ -1,13 +1,21 @@
 from concourse.bass import DstId, RemoteDMATransfer
 
 ROUNDS = 8
-PHASES = ROUNDS // 2
+C, RHO = 8, 26
+FLIGHTS = 1
+LANES = 2 * FLIGHTS
+W = C * RHO // 4
+
+_rows = list(range(0, 128 - RHO, RHO)) + [128 - RHO]
+SLABS = [(k0, r) for k0 in range(0, ROUNDS, C) for r in _rows]
+N = len(SLABS)
+assert N % FLIGHTS == 0
 
 SCRATCH = {
-    "own": ("dram", [2, 128, 64], "float32"),
-    "relay": ("dram", [2, 128, 64], "float32"),
+    "own": ("dram", [LANES * 2, 128, W], "float32"),
+    "relay": ("dram", [FLIGHTS * 2, 128, W], "float32"),
 }
-SEMAPHORES = ["loaded", "stored", "sent", "passing", "landed"]
+SEMAPHORES = ["sent", "loaded0", "loaded1", "stored0", "stored1", "passing0", "landed0"]
 
 LO, HI = 0x0F, 0xF0
 PER_CALL = 8
@@ -17,39 +25,73 @@ def rank_program(g, core, T, topo):
     if T.rank_of(core) is None:
         return
     h, place = topo.host(core), core % 128
+    loaded, stored = [T.sem.loaded0, T.sem.loaded1], [T.sem.stored0, T.sem.stored1]
+    passing, landed = [T.sem.passing0], [T.sem.landed0]
 
     def at(host):
         return host * 128 + place
 
-    def transfer(dst_core, mask, sem, src, dst):
+    def transfer(dst_core, mask, s, src, dst):
         rid, pid = topo.addr(dst_core, core)
-        return RemoteDMATransfer(dst_ids=[DstId(rid=rid, pnc=pid)], dma_engine_mask=mask, remote_sem=sem,
+        return RemoteDMATransfer(dst_ids=[DstId(rid=rid, pnc=pid)], dma_engine_mask=mask, remote_sem=s,
                                  src=src, dst=dst)
 
-    even_relay, odd_relay = (at(3), at(1)) if h % 2 == 0 else (at(0), at(2))
+    relay0, relay1 = (at(3), at(1)) if h % 2 == 0 else (at(0), at(2))
     side = h // 2
     client0, client1 = (at(1), at(3)) if h % 2 == 0 else (at(0), at(2))
-    parity = 0 if h in (0, 3) else 1
+    stream = 0 if h in (0, 3) else 1
 
-    for p in range(PHASES):
-        if p:
-            g.wait_ge(T.sem.landed, PER_CALL * p)
-            g.dma_start(T.y[2 * p - 2:2 * p], T.own[:]).then_inc(T.sem.stored, 16)
-            g.wait_ge(T.sem.stored, 16 * p)
-        g.dma_start(T.own[:], T.x[2 * p:2 * p + 2]).then_inc(T.sem.loaded, 16)
-        g.wait_ge(T.sem.loaded, 16 * (p + 1))
-        slot = (side + p) % 2
+    def slab(t, j):
+        k0, r = SLABS[j]
+        return t[k0:k0 + C, r:r + RHO, :]
+
+    def lane(j):
+        return T.own[2 * (j % LANES):2 * (j % LANES) + 2]
+
+    def load(j):
+        g.dma_start(lane(j), slab(T.x, j)).then_inc(loaded[j % LANES], 16)
+
+    def store(j):
+        g.dma_start(slab(T.y, j), lane(j)).then_inc(stored[j % LANES], 16)
+
+    def use(j):
+        return j // FLIGHTS
+
+    def send(j):
+        l, p = 2 * (j % LANES), 2 * (j % FLIGHTS)
+        slot = p + (side + use(j)) % 2
         g.remote_dma_fused([
-            transfer(even_relay, LO, T.sem.passing, T.own[0], T.relay[slot]),
-            transfer(odd_relay, HI, T.sem.passing, T.own[1], T.relay[slot]),
-        ], local_sem=T.sem.sent)
-        g.wait_ge(T.sem.passing, PER_CALL * (p + 1))
-        g.remote_dma_fused([
-            transfer(client1, LO, T.sem.landed, T.relay[p % 2], T.own[parity]),
-            transfer(client0, HI, T.sem.landed, T.relay[(p + 1) % 2], T.own[parity]),
+            transfer(relay0, LO, passing[j % FLIGHTS], T.own[l], T.relay[slot]),
+            transfer(relay1, HI, passing[j % FLIGHTS], T.own[l + 1], T.relay[slot]),
         ], local_sem=T.sem.sent)
 
-    g.wait_ge(T.sem.landed, PER_CALL * PHASES)
-    g.dma_start(T.y[ROUNDS - 2:ROUNDS], T.own[:]).then_inc(T.sem.stored, 16)
-    g.wait_ge(T.sem.stored, 16 * PHASES)
-    g.wait_ge(T.sem.sent, 2 * PER_CALL * PHASES)
+    def forward(j):
+        l, p = 2 * (j % LANES), 2 * (j % FLIGHTS)
+        g.remote_dma_fused([
+            transfer(client1, LO, landed[j % FLIGHTS], T.relay[p + use(j) % 2], T.own[l + stream]),
+            transfer(client0, HI, landed[j % FLIGHTS], T.relay[p + (use(j) + 1) % 2], T.own[l + stream]),
+        ], local_sem=T.sem.sent)
+
+    for j in range(min(LANES, N)):
+        load(j)
+    for s in range(0, N + FLIGHTS, FLIGHTS):
+        for j in range(s, s + FLIGHTS):
+            i = j - FLIGHTS
+            if i >= 0:
+                g.wait_ge(landed[i % FLIGHTS], PER_CALL * (use(i) + 1))
+            if j < N:
+                g.wait_ge(loaded[j % LANES], 16 * (j // LANES + 1))
+                send(j)
+            if i >= 0:
+                if i >= 1:
+                    g.wait_ge(stored[(i - 1) % LANES], 16 * ((i - 1) // LANES + 1))
+                store(i)
+        for j in range(s, min(s + FLIGHTS, N)):
+            g.wait_ge(passing[j % FLIGHTS], PER_CALL * (use(j) + 1))
+            forward(j)
+            i = j - FLIGHTS
+            if i >= 0 and i + LANES < N:
+                g.wait_ge(stored[i % LANES], 16 * (i // LANES + 1))
+                load(i + LANES)
+    g.wait_ge(stored[(N - 1) % LANES], 16 * ((N - 1) // LANES + 1))
+    g.wait_ge(T.sem.sent, 2 * PER_CALL * N)

@@ -1,21 +1,15 @@
 from concourse.bass import DstId, RemoteDMATransfer
 
-ROUNDS = 8
-C, RHO = 8, 26
-FLIGHTS = 1
-LANES = 2 * FLIGHTS
-W = C * RHO // 4
-
-_rows = list(range(0, 128 - RHO, RHO)) + [128 - RHO]
-SLABS = [(k0, r) for k0 in range(0, ROUNDS, C) for r in _rows]
-N = len(SLABS)
-assert N % FLIGHTS == 0
+ROWS = 26
+W = 26
+N = 5
+HALVES = 2
 
 SCRATCH = {
-    "own": ("dram", [LANES * 2, 128, W], "float32"),
-    "relay": ("dram", [FLIGHTS * 2, 128, W], "float32"),
+    "own": ("dram", [8, 128, W], "float32"),
+    "relay": ("dram", [4, 128, W], "float32"),
 }
-SEMAPHORES = ["sent", "loaded0", "loaded1", "stored0", "stored1", "passing0", "landed0"]
+SEMAPHORES = ["sent", "loaded0", "loaded1", "stored0", "stored1", "passing0", "passing1", "landed0", "landed1"]
 
 LO, HI = 0x0F, 0xF0
 PER_CALL = 8
@@ -26,72 +20,61 @@ def rank_program(g, core, T, topo):
         return
     h, place = topo.host(core), core % 128
     loaded, stored = [T.sem.loaded0, T.sem.loaded1], [T.sem.stored0, T.sem.stored1]
-    passing, landed = [T.sem.passing0], [T.sem.landed0]
+    passing, landed = [T.sem.passing0, T.sem.passing1], [T.sem.landed0, T.sem.landed1]
+    start = [min(ROWS * j, 128 - ROWS) for j in range(N)]
 
     def at(host):
         return host * 128 + place
 
-    def transfer(dst_core, mask, s, src, dst):
-        rid, pid = topo.addr(dst_core, core)
-        return RemoteDMATransfer(dst_ids=[DstId(rid=rid, pnc=pid)], dma_engine_mask=mask, remote_sem=s,
-                                 src=src, dst=dst)
+    def fused(moves, s):
+        transfers = []
+        for (dst_core, src, dst), mask in zip(moves, (LO, HI)):
+            rid, pid = topo.addr(dst_core, core)
+            transfers.append(RemoteDMATransfer(dst_ids=[DstId(rid=rid, pnc=pid)], dma_engine_mask=mask, remote_sem=s,
+                                               src=src, dst=dst))
+        g.remote_dma_fused(transfers, local_sem=T.sem.sent)
 
-    relay0, relay1 = (at(3), at(1)) if h % 2 == 0 else (at(0), at(2))
+    relays = (at(3), at(1)) if h % 2 == 0 else (at(0), at(2))
     side = h // 2
-    client0, client1 = (at(1), at(3)) if h % 2 == 0 else (at(0), at(2))
+    clients = (at(1), at(3)) if h % 2 == 0 else (at(0), at(2))
     stream = 0 if h in (0, 3) else 1
 
-    def slab(t, j):
-        k0, r = SLABS[j]
-        return t[k0:k0 + C, r:r + RHO, :]
-
     def lane(j):
-        return T.own[2 * (j % LANES):2 * (j % LANES) + 2]
+        return T.own[4 * (j % 2):4 * (j % 2) + 4]
 
     def load(j):
-        g.dma_start(lane(j), slab(T.x, j)).then_inc(loaded[j % LANES], 16)
+        g.dma_start(lane(j), T.x[:, start[j]:start[j] + ROWS, :]).then_inc(loaded[j % 2], 16)
 
     def store(j):
-        g.dma_start(slab(T.y, j), lane(j)).then_inc(stored[j % LANES], 16)
+        g.dma_start(T.y[:, start[j]:start[j] + ROWS, :], lane(j)).then_inc(stored[j % 2], 16)
 
-    def use(j):
-        return j // FLIGHTS
+    def send(j, q):
+        slot = (side + j) % 2
+        fused([(relays[s], T.own[4 * (j % 2) + 2 * s + q], T.relay[2 * q + slot]) for s in range(2)], passing[q])
 
-    def send(j):
-        l, p = 2 * (j % LANES), 2 * (j % FLIGHTS)
-        slot = p + (side + use(j)) % 2
-        g.remote_dma_fused([
-            transfer(relay0, LO, passing[j % FLIGHTS], T.own[l], T.relay[slot]),
-            transfer(relay1, HI, passing[j % FLIGHTS], T.own[l + 1], T.relay[slot]),
-        ], local_sem=T.sem.sent)
+    def forward(j, q):
+        fused([(clients[1 - c], T.relay[2 * q + (c + j) % 2], T.own[4 * (j % 2) + 2 * stream + q]) for c in range(2)],
+              landed[q])
 
-    def forward(j):
-        l, p = 2 * (j % LANES), 2 * (j % FLIGHTS)
-        g.remote_dma_fused([
-            transfer(client1, LO, landed[j % FLIGHTS], T.relay[p + use(j) % 2], T.own[l + stream]),
-            transfer(client0, HI, landed[j % FLIGHTS], T.relay[p + (use(j) + 1) % 2], T.own[l + stream]),
-        ], local_sem=T.sem.sent)
-
-    for j in range(min(LANES, N)):
-        load(j)
-    for s in range(0, N + FLIGHTS, FLIGHTS):
-        for j in range(s, s + FLIGHTS):
-            i = j - FLIGHTS
+    load(0)
+    load(1)
+    for j in range(N + 1):
+        i = j - 1
+        for q in range(HALVES):
             if i >= 0:
-                g.wait_ge(landed[i % FLIGHTS], PER_CALL * (use(i) + 1))
+                g.wait_ge(landed[q], PER_CALL * (i + 1))
             if j < N:
-                g.wait_ge(loaded[j % LANES], 16 * (j // LANES + 1))
-                send(j)
-            if i >= 0:
-                if i >= 1:
-                    g.wait_ge(stored[(i - 1) % LANES], 16 * ((i - 1) // LANES + 1))
-                store(i)
-        for j in range(s, min(s + FLIGHTS, N)):
-            g.wait_ge(passing[j % FLIGHTS], PER_CALL * (use(j) + 1))
-            forward(j)
-            i = j - FLIGHTS
-            if i >= 0 and i + LANES < N:
-                g.wait_ge(stored[i % LANES], 16 * (i // LANES + 1))
-                load(i + LANES)
-    g.wait_ge(stored[(N - 1) % LANES], 16 * ((N - 1) // LANES + 1))
-    g.wait_ge(T.sem.sent, 2 * PER_CALL * N)
+                if q == 0:
+                    g.wait_ge(loaded[j % 2], 16 * (j // 2 + 1))
+                send(j, q)
+        if i >= 0:
+            store(i)
+        if j < N:
+            for q in range(HALVES):
+                g.wait_ge(passing[q], PER_CALL * (j + 1))
+                forward(j, q)
+        if i >= 0:
+            g.wait_ge(stored[i % 2], 16 * (i // 2 + 1))
+            if i + 2 < N:
+                load(i + 2)
+    g.wait_ge(T.sem.sent, 2 * HALVES * PER_CALL * N)

from concourse.bass import DstId, RemoteDMATransfer

ROWS = 26
W = 26
N = 5
HALVES = 2

SCRATCH = {
    "own": ("dram", [8, 128, W], "float32"),
    "relay": ("dram", [4, 128, W], "float32"),
}
SEMAPHORES = ["sent", "loaded0", "loaded1", "stored0", "stored1", "passing0", "passing1", "landed0", "landed1"]

LO, HI = 0x0F, 0xF0
PER_CALL = 8


def rank_program(g, core, T, topo):
    if T.rank_of(core) is None:
        return
    h, place = topo.host(core), core % 128
    loaded, stored = [T.sem.loaded0, T.sem.loaded1], [T.sem.stored0, T.sem.stored1]
    passing, landed = [T.sem.passing0, T.sem.passing1], [T.sem.landed0, T.sem.landed1]
    start = [min(ROWS * j, 128 - ROWS) for j in range(N)]

    def at(host):
        return host * 128 + place

    def fused(moves, s):
        transfers = []
        for (dst_core, src, dst), mask in zip(moves, (LO, HI)):
            rid, pid = topo.addr(dst_core, core)
            transfers.append(RemoteDMATransfer(dst_ids=[DstId(rid=rid, pnc=pid)], dma_engine_mask=mask, remote_sem=s,
                                               src=src, dst=dst))
        g.remote_dma_fused(transfers, local_sem=T.sem.sent)

    relays = (at(3), at(1)) if h % 2 == 0 else (at(0), at(2))
    side = h // 2
    clients = (at(1), at(3)) if h % 2 == 0 else (at(0), at(2))
    stream = 0 if h in (0, 3) else 1

    def lane(j):
        return T.own[4 * (j % 2):4 * (j % 2) + 4]

    def load(j):
        g.dma_start(lane(j), T.x[:, start[j]:start[j] + ROWS, :]).then_inc(loaded[j % 2], 16)

    def store(j):
        g.dma_start(T.y[:, start[j]:start[j] + ROWS, :], lane(j)).then_inc(stored[j % 2], 16)

    def send(j, q):
        slot = (side + j) % 2
        fused([(relays[s], T.own[4 * (j % 2) + 2 * s + q], T.relay[2 * q + slot]) for s in range(2)], passing[q])

    def forward(j, q):
        fused([(clients[1 - c], T.relay[2 * q + (c + j) % 2], T.own[4 * (j % 2) + 2 * stream + q]) for c in range(2)],
              landed[q])

    load(0)
    load(1)
    for j in range(N + 1):
        i = j - 1
        for q in range(HALVES):
            if i >= 0:
                g.wait_ge(landed[q], PER_CALL * (i + 1))
            if j < N:
                if q == 0:
                    g.wait_ge(loaded[j % 2], 16 * (j // 2 + 1))
                send(j, q)
        if i >= 0:
            store(i)
        if j < N:
            for q in range(HALVES):
                g.wait_ge(passing[q], PER_CALL * (j + 1))
                forward(j, q)
        if i >= 0:
            g.wait_ge(stored[i % 2], 16 * (i // 2 + 1))
            if i + 2 < N:
                load(i + 2)
    g.wait_ge(T.sem.sent, 2 * HALVES * PER_CALL * N)
